import numpy as np
import ml_dtypes


def mxq(x, axis, fmt="e4m3"):
    dtype, down = {"e4m3": (ml_dtypes.float8_e4m3fn, 7), "e5m2": (ml_dtypes.float8_e5m2, 14)}[fmt]
    v = np.moveaxis(np.asarray(x, np.float32).astype(ml_dtypes.bfloat16).astype(np.float64), axis, -1)
    blocks = v.reshape(v.shape[:-1] + (-1, 32))
    amax = np.abs(blocks).max(-1, keepdims=True)
    byte = np.maximum(np.where(amax > 0, np.frexp(amax)[1] - 1 + 127, 0) - down, 1)
    scale = np.exp2(byte - 127.0)
    codes = (blocks / scale).astype(np.float32).astype(dtype).astype(np.float64)
    return np.moveaxis((codes * scale).reshape(v.shape), -1, axis)


WIDE = False


def mx_kscale(k):
    if not WIDE:
        return np.ones(k)
    levels = np.array([10, -10, 5, -5, 0])
    if k % 512:
        return np.exp2(np.random.permutation(np.resize(levels, k // 32))).repeat(32)
    a = np.empty((k // 512, 16))
    for p in range(k // 512):
        a[p, :8] = np.random.permutation(np.resize(levels, 8))
        for g in range(8):
            far = levels[np.abs(levels - a[p, g]) >= 10]
            a[p, g + 8] = far[np.random.randint(len(far))]
    return np.exp2(a.ravel()).repeat(32)


def f64(x):
    return np.asarray(x).astype(np.float64)


def striped(idx):
    return np.tile(np.asarray(idx).reshape(-1, 16).T, (8, 1)).astype(np.uint16)


def unstriped(offs):
    return offs[:16].T.reshape(-1).astype(np.int64)


E2M1 = np.array([0.0, 0.5, 1.0, 1.5, 2.0, 3.0, 4.0, 6.0, -0.0, -0.5, -1.0, -1.5, -2.0, -3.0, -4.0, -6.0])


def pack_weight(w, fmt):
    k, n = w.shape
    w = f64(np.asarray(w, np.float32).astype(ml_dtypes.bfloat16)).reshape(k // 32, 32, n)
    amax = np.abs(w).max(1)
    if fmt == "e4m3":
        byte = np.frexp(amax)[1] - 1 + 127 - 7
    else:
        mant, ex = np.frexp(amax / 6.0)
        byte = np.where(mant > 0.5, ex, ex - 1) + 127
    byte = np.clip(np.where(amax > 0, byte, 1), 1, 254)
    scaled = (w * np.exp2(127.0 - byte)[:, None, :]).reshape(k, n).astype(np.float32)
    by_word = np.ascontiguousarray(scaled.reshape(k // 512, 128, 4, n).transpose(0, 1, 3, 2))
    if fmt == "e4m3":
        words = by_word.astype(ml_dtypes.float8_e4m3fn).view(np.uint8)
    else:
        c = by_word.astype(ml_dtypes.float4_e2m1fn).view(np.uint8) & 0xF
        words = (c[..., 0::2] | (c[..., 1::2] << 4)).reshape(k // 512, 128, 2 * n)
    return np.ascontiguousarray(words), np.ascontiguousarray(byte.astype(np.uint8).reshape(k // 512, 16, n))


def unpack_weight(words, scales, fmt):
    g, _, n = scales.shape
    words = np.ascontiguousarray(words).reshape(g, 128, n, -1)
    if fmt == "e4m3":
        vals = words.view(ml_dtypes.float8_e4m3fn).astype(np.float64)
    else:
        nib = np.empty((g, 128, n, 4), np.uint8)
        nib[..., 0::2] = words & 0xF
        nib[..., 1::2] = words >> 4
        vals = E2M1[nib]
    vals = vals * np.repeat(np.exp2(scales.astype(np.float64) - 127.0), 8, axis=1)[..., None]
    return vals.transpose(0, 1, 3, 2).reshape(g * 512, n)


def bf(x):
    return np.asarray(x, np.float32).astype(ml_dtypes.bfloat16)


def planes(Y):
    r, m = Y.shape
    b = f64(bf(Y)).reshape(r // 32, 32, m)
    amax = np.abs(b).max(1)
    byte = np.clip(np.where(amax > 0, np.frexp(amax)[1] - 1 + 127 - 7, 1), 1, 254)
    codes = (b * np.exp2(127.0 - byte)[:, None, :]).reshape(r, m).astype(np.float32).astype(ml_dtypes.float8_e4m3fn).view(np.uint8)
    words = codes.reshape(r // 512, 128, 4, m).transpose(0, 1, 3, 2)
    return np.ascontiguousarray(words), np.ascontiguousarray(byte.astype(np.uint8).reshape(r // 512, 16, m))


K, T, J, B, L, N = 512, 2048, 1024, 128, 512, 512


def setup_inputs():
    n = np.random.standard_normal
    idx = (np.random.permutation(T // 8)[:J // 8, None] * 8 + np.arange(8)).reshape(-1)
    fk = mx_kscale(K)
    fl = mx_kscale(L)
    wcp = pack_weight(n((K, N)) * 1 / np.sqrt(K) * fk[:, None], "e4m3")
    xtp = pack_weight(n((L, T)) / fl[:, None], "e2m1")
    wap = pack_weight(n((L, N)) * 1 / np.sqrt(L) * fl[:, None], "e4m3")
    return {
        "xf": (n((K, T)) / fk[:, None]).astype(np.float32),
        "wc_words": wcp[0],
        "wc_scales": wcp[1],
        "xt_words": xtp[0],
        "xt_scales": xtp[1],
        "wa_words": wap[0],
        "wa_scales": wap[1],
        "ga": (np.random.uniform(0.4, 1.2, (1, J))).astype(np.float32),
        "offs": striped(idx),
    }


def reference(xf, wc_words, wc_scales, xt_words, xt_scales, wa_words, wa_scales, ga, offs):
    idx = unstriped(offs)
    wcu = unpack_weight(wc_words, wc_scales, "e4m3")
    xtu = unpack_weight(xt_words, xt_scales, "e2m1")
    wau = unpack_weight(wa_words, wa_scales, "e4m3")
    m1 = f64(xf)[:, idx].reshape(K, B, J // B).mean(axis=2)
    m2 = 2.0 * m1
    m2q = mxq(m2, 0, "e4m3")
    q = wcu.T @ m2q
    qr = np.repeat(q, J // B, axis=1)
    xtidxg = xtu[:, idx]
    p = wau.T @ xtidxg
    y = np.maximum(p + qr, 0.0) * f64(ga)
    words, scales = planes(y)
    return y, words, scales

@@ -1,0 +1,242 @@
+from contextlib import ExitStack
+
+import concourse.mybir as mybir
+from concourse.masks import make_identity
+
+K, T, J, B, L, N = 512, 2048, 1024, 128, 512, 512
+FLOPS = 2 * K * N * B + 2 * L * N * J
+
+F32 = mybir.dt.float32
+BF16 = mybir.dt.bfloat16
+I32 = mybir.dt.int32
+U32 = mybir.dt.uint32
+U16 = mybir.dt.uint16
+U8 = mybir.dt.uint8
+FP8X4 = mybir.dt.float8_e4m3fn_x4
+FP4X4 = mybir.dt.float4_e2m1fn_x4
+ALU = mybir.AluOpType
+
+P = 128
+PACK = 4
+RUN = 8
+HALF = J // 2
+QUARTER = J // 4
+LANES = 16
+
+
+def tile_moe_expert_with_block_context_pl_kernel(
+    tc, xf, wc_words, wc_scales, xt_words, xt_scales, wa_words, wa_scales, ga, offs, out_0, out_1, out_2
+):
+    nc = tc.nc
+    with ExitStack() as ctx:
+        keep = ctx.enter_context(tc.tile_pool(name="keep", bufs=1))
+        psum = ctx.enter_context(tc.psum_pool(name="psum", bufs=1))
+
+        def bank(number):
+            return psum.tile([P, 512], F32, name="bank%d" % number, tag="bank%d" % number)
+
+        def scale_plane(name, width):
+            plane = keep.tile([P, width], U8, name=name, align_bytes=64)
+            nc.vector.memset(plane[:].bitcast(I32), 0)
+            return plane
+
+        def load_scales(plane, scales):
+            rows = scales[0].bitcast(I32).rearrange("(quad q) c -> q quad c", q=4)
+            for q in range(4):
+                nc.sync.dma_start(plane[q:P:32, :].bitcast(I32), rows[q])
+
+        def load_words(name, words):
+            width = words.shape[1]
+            tile = keep.tile([P, width], U8, name=name, align_bytes=64)
+            nc.sync.dma_start(tile[:].bitcast(I32), words.bitcast(I32))
+            return tile
+
+        xt_plane = scale_plane("xt_plane", T)
+        wa_plane = scale_plane("wa_plane", N)
+        wc_plane = scale_plane("wc_plane", N)
+        identity = keep.tile([P, P], F32, name="identity")
+        make_identity(nc, identity[:])
+
+        offsets = keep.tile([P, J // LANES], U16, name="offsets")
+        nc.sync.dma_start(offsets[:], offs)
+        xt_table = load_words("xt_table", xt_words[0])
+        load_scales(xt_plane, xt_scales)
+        xf_rows = xf.rearrange("(p t) c -> p t c", t=PACK)
+        xf_table = []
+
+        def load_xf(t):
+            tile = keep.tile([P, T], F32, name="xf_table%d" % t)
+            nc.sync.dma_start(tile[:], xf_rows[:, t, :])
+            xf_table.append(tile)
+
+        load_xf(0)
+        wa_codes = load_words("wa_codes", wa_words[0].rearrange("p n t -> p (n t)"))
+        load_scales(wa_plane, wa_scales)
+        load_xf(1)
+        load_xf(2)
+        load_xf(3)
+        wc_codes = load_words("wc_codes", wc_words[0].rearrange("p n t -> p (n t)"))
+        load_scales(wc_plane, wc_scales)
+        gate = keep.tile([P, J], F32, name="gate")
+        nc.sync.dma_start(gate[:], ga[0].partition_broadcast(P))
+
+        def listed(first, count):
+            return offsets[:, first // LANES : (first + count) // LANES]
+
+        slot_words = keep.tile([P, 2 * J], U8, name="slot_words", align_bytes=64)
+        slot_plane = keep.tile([P, J], U8, name="slot_plane", align_bytes=64)
+        for g in range(2):
+            nc.vector.tensor_copy(
+                slot_words[:, 2 * HALF * g : 2 * HALF * (g + 1)].bitcast(U16),
+                xt_table[:].bitcast(U16).indirect(listed(HALF * g, HALF)),
+            )
+        nc.vector.tensor_copy(slot_plane[:], xt_plane[:].indirect(offsets[:]))
+
+        token_part = []
+        for i in range(J // P):
+            staged = bank(6 + i % 2)
+            nc.tensor.matmul_mx(
+                out=staged[:],
+                lhsT=slot_words[:, 2 * P * i : 2 * P * (i + 1)].bitcast(FP4X4),
+                lhsT_scale=slot_plane[:, P * i : P * (i + 1)],
+                rhs=wa_codes[:].bitcast(FP8X4),
+                rhs_scale=wa_plane[:],
+                start=True,
+                stop=True,
+            )
+            dealt = keep.tile([P, PACK, P], F32, name="token_part%d" % i)
+            nc.scalar.copy(dealt[:], staged[:].rearrange("j (m t) -> j t m", t=PACK))
+            token_part.append(dealt)
+
+        sums = {}
+
+        def open_sum(t, g):
+            sums[t, g] = bank(PACK * g + t)
+            for i in range(HALF // P):
+                nc.tensor.matmul(
+                    sums[t, g][:, P * i : P * (i + 1)],
+                    token_part[HALF // P * g + i][:, t, :],
+                    identity[:],
+                    is_transpose=True,
+                    start=(i == 0),
+                    stop=False,
+                )
+
+        for g in range(2):
+            for t in range(PACK):
+                if (t, g) != (PACK - 1, 1):
+                    open_sum(t, g)
+
+        block_sum = [keep.tile([P, PACK, B // 2, 1], F32, name="block_sum%d" % g) for g in range(2)]
+
+        def sum_blocks(t, g, picked):
+            nc.vector.tensor_reduce(
+                block_sum[g][:, t, :, 0],
+                picked.rearrange("p (b r) -> p b r", r=RUN),
+                axis=mybir.AxisListType.X,
+                op=ALU.add,
+            )
+
+        for t in range(PACK - 1):
+            picked = keep.tile([P, J], F32, name="picked%d" % t)
+            nc.vector.tensor_copy(picked[:], xf_table[t][:].indirect(offsets[:]))
+            for g in range(2):
+                sum_blocks(t, g, picked[:, HALF * g : HALF * (g + 1)])
+
+        context = []
+        for g in range(2):
+            picked = keep.tile([P, HALF], F32, name="picked_last%d" % g)
+            nc.vector.tensor_copy(picked[:], xf_table[PACK - 1][:].indirect(listed(HALF * g, HALF)))
+            sum_blocks(PACK - 1, g, picked[:])
+            m2 = keep.tile([P, B // 2, 2, PACK], BF16, name="m2_%d" % g, align_bytes=64)
+            nc.vector.tensor_scalar(
+                m2[:],
+                block_sum[g][:].rearrange("p t b o -> p b o t").to_broadcast([P, B // 2, 2, PACK]),
+                2.0 / RUN,
+                None,
+                ALU.mult,
+            )
+            m2_codes = keep.tile([P, P], U32, name="m2_codes%d" % g, align_bytes=64)
+            m2_plane = keep.tile([P, P], U8, name="m2_plane%d" % g, align_bytes=64)
+            nc.vector.quantize_mx(
+                out=m2_codes[:].bitcast(FP8X4), scales=m2_plane[:], in_=m2[:].rearrange("p b e t -> p (b e t)")
+            )
+            staged = bank(7)
+            nc.tensor.matmul_mx(
+                out=staged[:],
+                lhsT=m2_codes[:].bitcast(FP8X4),
+                lhsT_scale=m2_plane[:],
+                rhs=wc_codes[:].bitcast(FP8X4),
+                rhs_scale=wc_plane[:],
+                start=True,
+                stop=True,
+            )
+            dealt = keep.tile([P, PACK, P], F32, name="context%d" % g)
+            by_plane = staged[:].rearrange("c (m t) -> c t m", t=PACK)
+            nc.scalar.copy(dealt[:, 0:1, :], by_plane[:, 0:1, :])
+            nc.scalar.copy(dealt[:, 1:PACK, :], by_plane[:, 1:PACK, :])
+            context.append(dealt)
+
+        identity_pairs = identity[:].rearrange("p (b e) -> p b e", e=2)
+        out_rows = out_0.rearrange("(p t) j -> p t j", t=PACK)
+        y_codes = keep.tile([P, J], U32, name="y_codes", align_bytes=64)
+        y_plane = keep.tile([P, J], U8, name="y_plane", align_bytes=64)
+        out_words = out_1[0].rearrange("p c r -> p (c r)").bitcast(I32)
+        rounded = []
+
+        def close_sum(t, g):
+            by_pair = sums[t, g][:].rearrange("p (b r e) -> p r b e", r=RUN // 2, e=2)
+            for r in range(RUN // 2):
+                nc.tensor.matmul(
+                    by_pair[:, r],
+                    context[g][:, t, :],
+                    identity_pairs,
+                    is_transpose=True,
+                    start=False,
+                    stop=(r == RUN // 2 - 1),
+                )
+
+        def finish(u):
+            g, h = divmod(u, 2)
+            cols = slice(QUARTER * u, QUARTER * (u + 1))
+            y = keep.tile([P, PACK, QUARTER], F32, name="y%d" % u)
+            for t in range(PACK):
+                nc.vector.scalar_tensor_tensor(
+                    y[:, t, :], sums[t, g][:, QUARTER * h : QUARTER * (h + 1)], 0.0, gate[:, cols], ALU.max, ALU.mult
+                )
+            nc.sync.dma_start(out_rows[:, :, cols], y[:])
+            yb = keep.tile([P, QUARTER, PACK], BF16, name="rounded%d" % u, align_bytes=64)
+            dst = yb[:].rearrange("p (c i) t -> p c t i", i=4)
+            src = y[:].rearrange("p t (c i) -> p c t i", i=4)
+            if u < 3:
+                nc.scalar.copy(dst, src)
+            else:
+                nc.vector.tensor_copy(dst, src)
+            rounded.append(yb)
+
+        def quantise(u):
+            cols = slice(QUARTER * u, QUARTER * (u + 1))
+            nc.vector.quantize_mx(
+                out=y_codes[:, cols].bitcast(FP8X4),
+                scales=y_plane[:, cols],
+                in_=rounded[u][:].rearrange("p j t -> p (j t)"),
+            )
+            nc.sync.dma_start(out_words[:, cols], y_codes[:, cols].bitcast(I32))
+
+        for t in range(PACK):
+            close_sum(t, 0)
+        for t in range(PACK - 1):
+            close_sum(t, 1)
+        open_sum(PACK - 1, 1)
+        close_sum(PACK - 1, 1)
+        finish(0)
+        finish(1)
+        quantise(0)
+        finish(2)
+        quantise(1)
+        finish(3)
+        quantise(2)
+        quantise(3)
+        scale_rows = out_2[0].bitcast(I32).rearrange("(quad q) c -> q quad c", q=4)
+        for q in range(4):
+            nc.scalar.dma_start(scale_rows[q], y_plane[q:P:32, :].bitcast(I32))

@@ -15,6 +15,7 @@ U8 = mybir.dt.uint8
 FP8X4 = mybir.dt.float8_e4m3fn_x4
 FP4X4 = mybir.dt.float4_e2m1fn_x4
 ALU = mybir.AluOpType
+COPY = mybir.ActivationFunctionType.Copy
 
 P = 128
 PACK = 4
@@ -22,6 +23,7 @@ RUN = 8
 HALF = J // 2
 QUARTER = J // 4
 LANES = 16
+SCALAR_SHARE = 96
 
 
 def tile_moe_expert_with_block_context_pl_kernel(
@@ -40,10 +42,10 @@ def tile_moe_expert_with_block_context_pl_kernel(
             nc.vector.memset(plane[:].bitcast(I32), 0)
             return plane
 
-        def load_scales(plane, scales):
+        def load_scales(queue, plane, scales):
             rows = scales[0].bitcast(I32).rearrange("(quad q) c -> q quad c", q=4)
             for q in range(4):
-                nc.sync.dma_start(plane[q:P:32, :].bitcast(I32), rows[q])
+                queue.dma_start(plane[q:P:32, :].bitcast(I32), rows[q])
 
         def load_words(name, words):
             width = words.shape[1]
@@ -60,7 +62,7 @@ def tile_moe_expert_with_block_context_pl_kernel(
         offsets = keep.tile([P, J // LANES], U16, name="offsets")
         nc.sync.dma_start(offsets[:], offs)
         xt_table = load_words("xt_table", xt_words[0])
-        load_scales(xt_plane, xt_scales)
+        load_scales(nc.sync, xt_plane, xt_scales)
         xf_rows = xf.rearrange("(p t) c -> p t c", t=PACK)
         xf_table = []
 
@@ -70,15 +72,30 @@ def tile_moe_expert_with_block_context_pl_kernel(
             xf_table.append(tile)
 
         load_xf(0)
-        wa_codes = load_words("wa_codes", wa_words[0].rearrange("p n t -> p (n t)"))
-        load_scales(wa_plane, wa_scales)
         load_xf(1)
+        wa_codes = load_words("wa_codes", wa_words[0].rearrange("p n t -> p (n t)"))
+        load_scales(nc.sync, wa_plane, wa_scales)
         load_xf(2)
         load_xf(3)
         wc_codes = load_words("wc_codes", wc_words[0].rearrange("p n t -> p (n t)"))
-        load_scales(wc_plane, wc_scales)
+        load_scales(nc.sync, wc_plane, wc_scales)
+
+        gate_rows = keep.tile([P, P], F32, name="gate_rows")
+        nc.vector.memset(gate_rows[:], 0.0)
+        nc.scalar.dma_start(gate_rows[0 : J // P, :], ga[0].rearrange("(i c) -> i c", c=P))
+        turned = bank(7)
+        nc.tensor.transpose(turned[:, 0:P], gate_rows[:], identity[:])
+        gate_columns = keep.tile([P, J // P], F32, name="gate_columns")
+        nc.scalar.activation(gate_columns[:], turned[:, 0 : J // P], COPY)
         gate = keep.tile([P, J], F32, name="gate")
-        nc.sync.dma_start(gate[:], ga[0].partition_broadcast(P))
+        for g in range(2):
+            spread = bank(6 + g)
+            for i in range(HALF // P):
+                column = HALF // P * g + i
+                nc.tensor.transpose(
+                    spread[:, P * i : P * (i + 1)], gate_columns[:, column : column + 1].to_broadcast([P, P]), identity[:]
+                )
+            nc.scalar.copy(gate[:, HALF * g : HALF * (g + 1)], spread[:])
 
         def listed(first, count):
             return offsets[:, first // LANES : (first + count) // LANES]
@@ -90,6 +107,7 @@ def tile_moe_expert_with_block_context_pl_kernel(
                 slot_words[:, 2 * HALF * g : 2 * HALF * (g + 1)].bitcast(U16),
                 xt_table[:].bitcast(U16).indirect(listed(HALF * g, HALF)),
             )
+
         nc.vector.tensor_copy(slot_plane[:], xt_plane[:].indirect(offsets[:]))
 
         token_part = []
@@ -105,7 +123,7 @@ def tile_moe_expert_with_block_context_pl_kernel(
                 stop=True,
             )
             dealt = keep.tile([P, PACK, P], F32, name="token_part%d" % i)
-            nc.scalar.copy(dealt[:], staged[:].rearrange("j (m t) -> j t m", t=PACK))
+            nc.scalar.activation(dealt[:], staged[:].rearrange("j (m t) -> j t m", t=PACK), COPY)
             token_part.append(dealt)
 
         sums = {}
@@ -127,11 +145,11 @@ def tile_moe_expert_with_block_context_pl_kernel(
                 if (t, g) != (PACK - 1, 1):
                     open_sum(t, g)
 
-        block_sum = [keep.tile([P, PACK, B // 2, 1], F32, name="block_sum%d" % g) for g in range(2)]
+        block_sum = keep.tile([P, 2, PACK, B // 2, 1], F32, name="block_sum")
 
         def sum_blocks(t, g, picked):
             nc.vector.tensor_reduce(
-                block_sum[g][:, t, :, 0],
+                block_sum[:, g, t, :, 0],
                 picked.rearrange("p (b r) -> p b r", r=RUN),
                 axis=mybir.AxisListType.X,
                 op=ALU.add,
@@ -140,28 +158,47 @@ def tile_moe_expert_with_block_context_pl_kernel(
         for t in range(PACK - 1):
             picked = keep.tile([P, J], F32, name="picked%d" % t)
             nc.vector.tensor_copy(picked[:], xf_table[t][:].indirect(offsets[:]))
-            for g in range(2):
-                sum_blocks(t, g, picked[:, HALF * g : HALF * (g + 1)])
+            if t < 2:
+                fours = keep.tile([P, 4, B], F32, name="fours%d" % t)
+                twos = keep.tile([P, 2, B], F32, name="twos%d" % t)
+                runs = picked[:].rearrange("p (b h r) -> p h r b", h=2, r=RUN // 2)
+                nc.gpsimd.tensor_tensor(fours[:], runs[:, 0], runs[:, 1], ALU.add)
+                nc.gpsimd.tensor_tensor(twos[:], fours[:, 0:2, :], fours[:, 2:4, :], ALU.add)
+                nc.gpsimd.tensor_tensor(
+                    block_sum[:, :, t, :, 0],
+                    twos[:, 0, :].rearrange("p (g b) -> p g b", g=2),
+                    twos[:, 1, :].rearrange("p (g b) -> p g b", g=2),
+                    ALU.add,
+                )
+            else:
+                nc.vector.tensor_reduce(
+                    block_sum[:, :, t, :, 0],
+                    picked[:].rearrange("p (g b r) -> p g b r", g=2, r=RUN),
+                    axis=mybir.AxisListType.X,
+                    op=ALU.add,
+                )
 
         context = []
+        means = []
         for g in range(2):
             picked = keep.tile([P, HALF], F32, name="picked_last%d" % g)
             nc.vector.tensor_copy(picked[:], xf_table[PACK - 1][:].indirect(listed(HALF * g, HALF)))
             sum_blocks(PACK - 1, g, picked[:])
             m2 = keep.tile([P, B // 2, 2, PACK], BF16, name="m2_%d" % g, align_bytes=64)
-            nc.vector.tensor_scalar(
-                m2[:],
-                block_sum[g][:].rearrange("p t b o -> p b o t").to_broadcast([P, B // 2, 2, PACK]),
-                2.0 / RUN,
-                None,
-                ALU.mult,
-            )
+            doubled = block_sum[:, g].rearrange("p t b o -> p b o t").to_broadcast([P, B // 2, 2, PACK])
+            if g == 0:
+                nc.scalar.activation(m2[:], doubled, COPY, scale=2.0 / RUN)
+            else:
+                nc.vector.tensor_scalar(m2[:], doubled, 2.0 / RUN, None, ALU.mult)
             m2_codes = keep.tile([P, P], U32, name="m2_codes%d" % g, align_bytes=64)
             m2_plane = keep.tile([P, P], U8, name="m2_plane%d" % g, align_bytes=64)
             nc.vector.quantize_mx(
                 out=m2_codes[:].bitcast(FP8X4), scales=m2_plane[:], in_=m2[:].rearrange("p b e t -> p (b e t)")
             )
-            staged = bank(7)
+            means.append((m2_codes, m2_plane))
+
+        def multiply_means(g, staged):
+            m2_codes, m2_plane = means[g]
             nc.tensor.matmul_mx(
                 out=staged[:],
                 lhsT=m2_codes[:].bitcast(FP8X4),
@@ -196,23 +233,37 @@ def tile_moe_expert_with_block_context_pl_kernel(
                     stop=(r == RUN // 2 - 1),
                 )
 
-        def finish(u):
-            g, h = divmod(u, 2)
+        def gated(dst, t, cols):
+            g = cols.start // HALF
+            nc.vector.scalar_tensor_tensor(
+                dst, sums[t, g][:, cols.start - HALF * g : cols.stop - HALF * g], 0.0, gate[:, cols], ALU.max, ALU.mult
+            )
+
+        def round_columns(copy, dst, src):
+            copy(dst.rearrange("p (c i) t -> p c t i", i=4), src.rearrange("p t (c i) -> p c t i", i=4))
+
+        def round_quarter(u, y):
+            yb = keep.tile([P, QUARTER, PACK], BF16, name="rounded%d" % u, align_bytes=64)
+            if u < 3:
+                round_columns(nc.scalar.copy, yb[:], y)
+            else:
+                round_columns(nc.scalar.copy, yb[:, 0:SCALAR_SHARE, :], y[:, :, 0:SCALAR_SHARE])
+                round_columns(nc.vector.tensor_copy, yb[:, SCALAR_SHARE:QUARTER, :], y[:, :, SCALAR_SHARE:QUARTER])
+            rounded.append(yb)
+
+        y_first = keep.tile([P, PACK, HALF], F32, name="y_first")
+
+        def finish_first(t):
+            gated(y_first[:, t, :], t, slice(0, HALF))
+            nc.sync.dma_start(out_rows[:, t, 0:HALF], y_first[:, t, :])
+
+        def finish_quarter(u):
             cols = slice(QUARTER * u, QUARTER * (u + 1))
             y = keep.tile([P, PACK, QUARTER], F32, name="y%d" % u)
             for t in range(PACK):
-                nc.vector.scalar_tensor_tensor(
-                    y[:, t, :], sums[t, g][:, QUARTER * h : QUARTER * (h + 1)], 0.0, gate[:, cols], ALU.max, ALU.mult
-                )
+                gated(y[:, t, :], t, cols)
             nc.sync.dma_start(out_rows[:, :, cols], y[:])
-            yb = keep.tile([P, QUARTER, PACK], BF16, name="rounded%d" % u, align_bytes=64)
-            dst = yb[:].rearrange("p (c i) t -> p c t i", i=4)
-            src = y[:].rearrange("p t (c i) -> p c t i", i=4)
-            if u < 3:
-                nc.scalar.copy(dst, src)
-            else:
-                nc.vector.tensor_copy(dst, src)
-            rounded.append(yb)
+            round_quarter(u, y[:])
 
         def quantise(u):
             cols = slice(QUARTER * u, QUARTER * (u + 1))
@@ -223,20 +274,25 @@ def tile_moe_expert_with_block_context_pl_kernel(
             )
             nc.sync.dma_start(out_words[:, cols], y_codes[:, cols].bitcast(I32))
 
+        multiply_means(0, bank(7))
+        multiply_means(1, bank(7))
         for t in range(PACK):
             close_sum(t, 0)
         for t in range(PACK - 1):
             close_sum(t, 1)
         open_sum(PACK - 1, 1)
         close_sum(PACK - 1, 1)
-        finish(0)
-        finish(1)
+        for t in range(PACK):
+            finish_first(t)
+        for u in range(2):
+            round_quarter(u, y_first[:, :, QUARTER * u : QUARTER * (u + 1)])
+        finish_quarter(2)
         quantise(0)
-        finish(2)
         quantise(1)
-        finish(3)
+        finish_quarter(3)
         quantise(2)
         quantise(3)
         scale_rows = out_2[0].bitcast(I32).rearrange("(quad q) c -> q quad c", q=4)
         for q in range(4):
-            nc.scalar.dma_start(scale_rows[q], y_plane[q:P:32, :].bitcast(I32))
+            queue = nc.scalar if q < 3 else nc.sync
+            queue.dma_start(scale_rows[q], y_plane[q:P:32, :].bitcast(I32))

from contextlib import ExitStack

import concourse.mybir as mybir
from concourse.masks import make_identity

K, T, J, B, L, N = 512, 2048, 1024, 128, 512, 512
FLOPS = 2 * K * N * B + 2 * L * N * J

F32 = mybir.dt.float32
BF16 = mybir.dt.bfloat16
I32 = mybir.dt.int32
U32 = mybir.dt.uint32
U16 = mybir.dt.uint16
U8 = mybir.dt.uint8
FP8X4 = mybir.dt.float8_e4m3fn_x4
FP4X4 = mybir.dt.float4_e2m1fn_x4
ALU = mybir.AluOpType
COPY = mybir.ActivationFunctionType.Copy

P = 128
PACK = 4
RUN = 8
HALF = J // 2
QUARTER = J // 4
LANES = 16
SCALAR_SHARE = 96


def tile_moe_expert_with_block_context_pl_kernel(
    tc, xf, wc_words, wc_scales, xt_words, xt_scales, wa_words, wa_scales, ga, offs, out_0, out_1, out_2
):
    nc = tc.nc
    with ExitStack() as ctx:
        keep = ctx.enter_context(tc.tile_pool(name="keep", bufs=1))
        psum = ctx.enter_context(tc.psum_pool(name="psum", bufs=1))

        def bank(number):
            return psum.tile([P, 512], F32, name="bank%d" % number, tag="bank%d" % number)

        def scale_plane(name, width):
            plane = keep.tile([P, width], U8, name=name, align_bytes=64)
            nc.vector.memset(plane[:].bitcast(I32), 0)
            return plane

        def load_scales(queue, plane, scales):
            rows = scales[0].bitcast(I32).rearrange("(quad q) c -> q quad c", q=4)
            for q in range(4):
                queue.dma_start(plane[q:P:32, :].bitcast(I32), rows[q])

        def load_words(name, words):
            width = words.shape[1]
            tile = keep.tile([P, width], U8, name=name, align_bytes=64)
            nc.sync.dma_start(tile[:].bitcast(I32), words.bitcast(I32))
            return tile

        xt_plane = scale_plane("xt_plane", T)
        wa_plane = scale_plane("wa_plane", N)
        wc_plane = scale_plane("wc_plane", N)
        identity = keep.tile([P, P], F32, name="identity")
        make_identity(nc, identity[:])

        offsets = keep.tile([P, J // LANES], U16, name="offsets")
        nc.sync.dma_start(offsets[:], offs)
        xt_table = load_words("xt_table", xt_words[0])
        load_scales(nc.sync, xt_plane, xt_scales)
        xf_rows = xf.rearrange("(p t) c -> p t c", t=PACK)
        xf_table = []

        def load_xf(t):
            tile = keep.tile([P, T], F32, name="xf_table%d" % t)
            nc.sync.dma_start(tile[:], xf_rows[:, t, :])
            xf_table.append(tile)

        load_xf(0)
        load_xf(1)
        wa_codes = load_words("wa_codes", wa_words[0].rearrange("p n t -> p (n t)"))
        load_scales(nc.sync, wa_plane, wa_scales)
        load_xf(2)
        load_xf(3)
        wc_codes = load_words("wc_codes", wc_words[0].rearrange("p n t -> p (n t)"))
        load_scales(nc.sync, wc_plane, wc_scales)

        gate_rows = keep.tile([P, P], F32, name="gate_rows")
        nc.vector.memset(gate_rows[:], 0.0)
        nc.scalar.dma_start(gate_rows[0 : J // P, :], ga[0].rearrange("(i c) -> i c", c=P))
        turned = bank(7)
        nc.tensor.transpose(turned[:, 0:P], gate_rows[:], identity[:])
        gate_columns = keep.tile([P, J // P], F32, name="gate_columns")
        nc.scalar.activation(gate_columns[:], turned[:, 0 : J // P], COPY)
        gate = keep.tile([P, J], F32, name="gate")
        for g in range(2):
            spread = bank(6 + g)
            for i in range(HALF // P):
                column = HALF // P * g + i
                nc.tensor.transpose(
                    spread[:, P * i : P * (i + 1)], gate_columns[:, column : column + 1].to_broadcast([P, P]), identity[:]
                )
            nc.scalar.copy(gate[:, HALF * g : HALF * (g + 1)], spread[:])

        def listed(first, count):
            return offsets[:, first // LANES : (first + count) // LANES]

        slot_words = keep.tile([P, 2 * J], U8, name="slot_words", align_bytes=64)
        slot_plane = keep.tile([P, J], U8, name="slot_plane", align_bytes=64)
        for g in range(2):
            nc.vector.tensor_copy(
                slot_words[:, 2 * HALF * g : 2 * HALF * (g + 1)].bitcast(U16),
                xt_table[:].bitcast(U16).indirect(listed(HALF * g, HALF)),
            )

        nc.vector.tensor_copy(slot_plane[:], xt_plane[:].indirect(offsets[:]))

        token_part = []
        for i in range(J // P):
            staged = bank(6 + i % 2)
            nc.tensor.matmul_mx(
                out=staged[:],
                lhsT=slot_words[:, 2 * P * i : 2 * P * (i + 1)].bitcast(FP4X4),
                lhsT_scale=slot_plane[:, P * i : P * (i + 1)],
                rhs=wa_codes[:].bitcast(FP8X4),
                rhs_scale=wa_plane[:],
                start=True,
                stop=True,
            )
            dealt = keep.tile([P, PACK, P], F32, name="token_part%d" % i)
            nc.scalar.activation(dealt[:], staged[:].rearrange("j (m t) -> j t m", t=PACK), COPY)
            token_part.append(dealt)

        sums = {}

        def open_sum(t, g):
            sums[t, g] = bank(PACK * g + t)
            for i in range(HALF // P):
                nc.tensor.matmul(
                    sums[t, g][:, P * i : P * (i + 1)],
                    token_part[HALF // P * g + i][:, t, :],
                    identity[:],
                    is_transpose=True,
                    start=(i == 0),
                    stop=False,
                )

        for g in range(2):
            for t in range(PACK):
                if (t, g) != (PACK - 1, 1):
                    open_sum(t, g)

        block_sum = keep.tile([P, 2, PACK, B // 2, 1], F32, name="block_sum")

        def sum_blocks(t, g, picked):
            nc.vector.tensor_reduce(
                block_sum[:, g, t, :, 0],
                picked.rearrange("p (b r) -> p b r", r=RUN),
                axis=mybir.AxisListType.X,
                op=ALU.add,
            )

        for t in range(PACK - 1):
            picked = keep.tile([P, J], F32, name="picked%d" % t)
            nc.vector.tensor_copy(picked[:], xf_table[t][:].indirect(offsets[:]))
            if t < 2:
                fours = keep.tile([P, 4, B], F32, name="fours%d" % t)
                twos = keep.tile([P, 2, B], F32, name="twos%d" % t)
                runs = picked[:].rearrange("p (b h r) -> p h r b", h=2, r=RUN // 2)
                nc.gpsimd.tensor_tensor(fours[:], runs[:, 0], runs[:, 1], ALU.add)
                nc.gpsimd.tensor_tensor(twos[:], fours[:, 0:2, :], fours[:, 2:4, :], ALU.add)
                nc.gpsimd.tensor_tensor(
                    block_sum[:, :, t, :, 0],
                    twos[:, 0, :].rearrange("p (g b) -> p g b", g=2),
                    twos[:, 1, :].rearrange("p (g b) -> p g b", g=2),
                    ALU.add,
                )
            else:
                nc.vector.tensor_reduce(
                    block_sum[:, :, t, :, 0],
                    picked[:].rearrange("p (g b r) -> p g b r", g=2, r=RUN),
                    axis=mybir.AxisListType.X,
                    op=ALU.add,
                )

        context = []
        means = []
        for g in range(2):
            picked = keep.tile([P, HALF], F32, name="picked_last%d" % g)
            nc.vector.tensor_copy(picked[:], xf_table[PACK - 1][:].indirect(listed(HALF * g, HALF)))
            sum_blocks(PACK - 1, g, picked[:])
            m2 = keep.tile([P, B // 2, 2, PACK], BF16, name="m2_%d" % g, align_bytes=64)
            doubled = block_sum[:, g].rearrange("p t b o -> p b o t").to_broadcast([P, B // 2, 2, PACK])
            if g == 0:
                nc.scalar.activation(m2[:], doubled, COPY, scale=2.0 / RUN)
            else:
                nc.vector.tensor_scalar(m2[:], doubled, 2.0 / RUN, None, ALU.mult)
            m2_codes = keep.tile([P, P], U32, name="m2_codes%d" % g, align_bytes=64)
            m2_plane = keep.tile([P, P], U8, name="m2_plane%d" % g, align_bytes=64)
            nc.vector.quantize_mx(
                out=m2_codes[:].bitcast(FP8X4), scales=m2_plane[:], in_=m2[:].rearrange("p b e t -> p (b e t)")
            )
            means.append((m2_codes, m2_plane))

        def multiply_means(g, staged):
            m2_codes, m2_plane = means[g]
            nc.tensor.matmul_mx(
                out=staged[:],
                lhsT=m2_codes[:].bitcast(FP8X4),
                lhsT_scale=m2_plane[:],
                rhs=wc_codes[:].bitcast(FP8X4),
                rhs_scale=wc_plane[:],
                start=True,
                stop=True,
            )
            dealt = keep.tile([P, PACK, P], F32, name="context%d" % g)
            by_plane = staged[:].rearrange("c (m t) -> c t m", t=PACK)
            nc.scalar.copy(dealt[:, 0:1, :], by_plane[:, 0:1, :])
            nc.scalar.copy(dealt[:, 1:PACK, :], by_plane[:, 1:PACK, :])
            context.append(dealt)

        identity_pairs = identity[:].rearrange("p (b e) -> p b e", e=2)
        out_rows = out_0.rearrange("(p t) j -> p t j", t=PACK)
        y_codes = keep.tile([P, J], U32, name="y_codes", align_bytes=64)
        y_plane = keep.tile([P, J], U8, name="y_plane", align_bytes=64)
        out_words = out_1[0].rearrange("p c r -> p (c r)").bitcast(I32)
        rounded = []

        def close_sum(t, g):
            by_pair = sums[t, g][:].rearrange("p (b r e) -> p r b e", r=RUN // 2, e=2)
            for r in range(RUN // 2):
                nc.tensor.matmul(
                    by_pair[:, r],
                    context[g][:, t, :],
                    identity_pairs,
                    is_transpose=True,
                    start=False,
                    stop=(r == RUN // 2 - 1),
                )

        def gated(dst, t, cols):
            g = cols.start // HALF
            nc.vector.scalar_tensor_tensor(
                dst, sums[t, g][:, cols.start - HALF * g : cols.stop - HALF * g], 0.0, gate[:, cols], ALU.max, ALU.mult
            )

        def round_columns(copy, dst, src):
            copy(dst.rearrange("p (c i) t -> p c t i", i=4), src.rearrange("p t (c i) -> p c t i", i=4))

        def round_quarter(u, y):
            yb = keep.tile([P, QUARTER, PACK], BF16, name="rounded%d" % u, align_bytes=64)
            if u < 3:
                round_columns(nc.scalar.copy, yb[:], y)
            else:
                round_columns(nc.scalar.copy, yb[:, 0:SCALAR_SHARE, :], y[:, :, 0:SCALAR_SHARE])
                round_columns(nc.vector.tensor_copy, yb[:, SCALAR_SHARE:QUARTER, :], y[:, :, SCALAR_SHARE:QUARTER])
            rounded.append(yb)

        y_first = keep.tile([P, PACK, HALF], F32, name="y_first")

        def finish_first(t):
            gated(y_first[:, t, :], t, slice(0, HALF))
            nc.sync.dma_start(out_rows[:, t, 0:HALF], y_first[:, t, :])

        def finish_quarter(u):
            cols = slice(QUARTER * u, QUARTER * (u + 1))
            y = keep.tile([P, PACK, QUARTER], F32, name="y%d" % u)
            for t in range(PACK):
                gated(y[:, t, :], t, cols)
            nc.sync.dma_start(out_rows[:, :, cols], y[:])
            round_quarter(u, y[:])

        def quantise(u):
            cols = slice(QUARTER * u, QUARTER * (u + 1))
            nc.vector.quantize_mx(
                out=y_codes[:, cols].bitcast(FP8X4),
                scales=y_plane[:, cols],
                in_=rounded[u][:].rearrange("p j t -> p (j t)"),
            )
            nc.sync.dma_start(out_words[:, cols], y_codes[:, cols].bitcast(I32))

        multiply_means(0, bank(7))
        multiply_means(1, bank(7))
        for t in range(PACK):
            close_sum(t, 0)
        for t in range(PACK - 1):
            close_sum(t, 1)
        open_sum(PACK - 1, 1)
        close_sum(PACK - 1, 1)
        for t in range(PACK):
            finish_first(t)
        for u in range(2):
            round_quarter(u, y_first[:, :, QUARTER * u : QUARTER * (u + 1)])
        finish_quarter(2)
        quantise(0)
        quantise(1)
        finish_quarter(3)
        quantise(2)
        quantise(3)
        scale_rows = out_2[0].bitcast(I32).rearrange("(quad q) c -> q quad c", q=4)
        for q in range(4):
            queue = nc.scalar if q < 3 else nc.sync
            queue.dma_start(scale_rows[q], y_plane[q:P:32, :].bitcast(I32))
